import numpy as np
import ml_dtypes


def mxq(x, axis, fmt="e4m3"):
    dtype, down = {"e4m3": (ml_dtypes.float8_e4m3fn, 7), "e5m2": (ml_dtypes.float8_e5m2, 14)}[fmt]
    v = np.moveaxis(np.asarray(x, np.float32).astype(ml_dtypes.bfloat16).astype(np.float64), axis, -1)
    blocks = v.reshape(v.shape[:-1] + (-1, 32))
    amax = np.abs(blocks).max(-1, keepdims=True)
    byte = np.maximum(np.where(amax > 0, np.frexp(amax)[1] - 1 + 127, 0) - down, 1)
    scale = np.exp2(byte - 127.0)
    codes = (blocks / scale).astype(np.float32).astype(dtype).astype(np.float64)
    return np.moveaxis((codes * scale).reshape(v.shape), -1, axis)


WIDE = False


def mx_kscale(k):
    if not WIDE:
        return np.ones(k)
    levels = np.array([10, -10, 5, -5, 0])
    if k % 512:
        return np.exp2(np.random.permutation(np.resize(levels, k // 32))).repeat(32)
    a = np.empty((k // 512, 16))
    for p in range(k // 512):
        a[p, :8] = np.random.permutation(np.resize(levels, 8))
        for g in range(8):
            far = levels[np.abs(levels - a[p, g]) >= 10]
            a[p, g + 8] = far[np.random.randint(len(far))]
    return np.exp2(a.ravel()).repeat(32)


def f64(x):
    return np.asarray(x).astype(np.float64)


def striped(idx):
    return np.tile(idx.reshape(-1, 16).T, (8, 1)).astype(np.uint16)


def unstriped(offs):
    return offs[:16].T.reshape(-1).astype(np.int64)


def striped8(idx):
    return np.concatenate([x.reshape(-1, 16).T for x in idx]).astype(np.uint16)


def runs(offs, k):
    lists = np.stack([offs[16 * r : 16 * r + 16].T.reshape(-1) for r in range(8)]).astype(np.int64)
    return lists[np.arange(k) % 512 // 64]


def pack_weight(w):
    k, n = w.shape
    w = f64(np.asarray(w, np.float32).astype(ml_dtypes.bfloat16)).reshape(k // 32, 32, n)
    amax = np.abs(w).max(1)
    byte = np.clip(np.where(amax > 0, np.frexp(amax)[1] - 1 + 127 - 7, 1), 1, 254)
    scaled = (w * np.exp2(127.0 - byte)[:, None, :]).reshape(k, n).astype(np.float32)
    words = np.ascontiguousarray(scaled.reshape(k // 512, 128, 4, n).transpose(0, 1, 3, 2)).astype(ml_dtypes.float8_e4m3fn).view(np.uint8)
    return words, np.ascontiguousarray(byte.astype(np.uint8).reshape(k // 512, 16, n))


def unpack_weight(words, scales):
    g, p, n, _ = words.shape
    vals = np.ascontiguousarray(words).view(ml_dtypes.float8_e4m3fn).astype(np.float64) * np.repeat(np.exp2(scales.astype(np.float64) - 127.0), 8, axis=1)[..., None]
    return vals.transpose(0, 1, 3, 2).reshape(g * 512, n)


K, T, S, N, H = 512, 2048, 512, 512, 512
P = 2 ** 7


def setup_inputs():
    n = np.random.standard_normal
    s = mx_kscale(K)[:, None]
    u = mx_kscale(H)
    packed_xT = pack_weight(n((K, T)) * s)
    return {
        "x_words": packed_xT[0],
        "x_scales": packed_xT[1],
        "w1": (n((K, H)) / np.sqrt(K) / s * u).astype(np.float32),
        "ga": np.tile(np.random.uniform(0.2, 1.0, S), (P, 1)).astype(np.float32),
        "gb": np.tile(np.random.uniform(0.2, 1.0, S), (P, 1)).astype(np.float32),
        "w2": (n((H, N)) / np.sqrt(3 * H) / u[:, None]).astype(np.float32),
        "w3": (n((H, N)) / np.sqrt(3 * H) / u[:, None]).astype(np.float32),
        "w4": (n((H, N)) / np.sqrt(3 * H) / u[:, None]).astype(np.float32),
        "offs": striped(np.random.permutation(T)[:S]),
        "p1": striped8(np.stack([np.random.permutation(S) for _ in range(8)])),
        "p2": striped8(np.stack([np.random.permutation(S) for _ in range(8)])),
    }


def reference(x_words, x_scales, w1, ga, gb, w2, w3, w4, offs, p1, p2):
    xq = unpack_weight(x_words, x_scales)[:, unstriped(offs)]
    y = mxq(f64(w1), 0, "e4m3").T @ xq
    h = f64(ga)[:1] * (y[np.arange(H)[:, None], runs(p1, H)]) + f64(gb)[:1] * (y[np.arange(H)[:, None], runs(p2, H)])
    z = 2.0 * (f64(ga)[:1] * (h[np.arange(H)[:, None], runs(p1, H)]) + f64(gb)[:1] * (h[np.arange(H)[:, None], runs(p2, H)])) - y
    return mxq(f64(w2), 0, "e4m3").T @ mxq(y, 0, "e4m3") + mxq(f64(w3), 0, "e4m3").T @ mxq(h, 0, "e4m3") + mxq(f64(w4), 0, "e4m3").T @ mxq(z, 0, "e4m3")

@@ -1,0 +1,303 @@
+from contextlib import ExitStack
+
+import concourse.mybir as mybir
+from concourse.masks import make_identity
+
+K, T, S, N, H = 512, 2048, 512, 512, 512
+FLOPS = 4 * 2 * 512 * 512 * 512
+
+F32 = mybir.dt.float32
+BF16 = mybir.dt.bfloat16
+I32 = mybir.dt.int32
+U32 = mybir.dt.uint32
+U16 = mybir.dt.uint16
+U8 = mybir.dt.uint8
+FP8X4 = mybir.dt.float8_e4m3fn_x4
+MULT = mybir.AluOpType.mult
+ADD = mybir.AluOpType.add
+COPY = mybir.ActivationFunctionType.Copy
+
+P = 128
+PACK = 4
+HALF = S // 2
+PE_PLANES = (0, 1, 2, 3)
+SUBTRACT = mybir.AluOpType.subtract
+Z_SLICES = ((0, 256), (256, 384), (384, 512))
+
+
+def tile_picked_cheb3_none_p_kernel(
+    tc, x_words, x_scales, w1, ga, gb, w2, w3, w4, offs, p1, p2, out
+):
+    nc = tc.nc
+    with ExitStack() as ctx:
+        lists = ctx.enter_context(tc.tile_pool(name="lists", bufs=1))
+        sb = ctx.enter_context(tc.tile_pool(name="sb", bufs=1))
+        ps = ctx.enter_context(tc.psum_pool(name="ps", bufs=1))
+
+        def sbuf(shape, dtype, name, tag=None):
+            return sb.tile(shape, dtype, name=name, tag=tag or name, align_bytes=64)
+
+        def bank(shape, name, tag, bufs=1):
+            return ps.tile(shape, F32, name=name, tag=tag, bufs=bufs)
+
+        def cols(tile, lo, hi):
+            return tile[:, lo // 16 : hi // 16]
+
+        def quantize(codes, scales, values):
+            nc.vector.quantize_mx(out=codes.bitcast(FP8X4), scales=scales, in_=values)
+
+        def matmul_mx(acc, lhs, lhs_cols, rhs, rhs_cols, start, stop):
+            nc.tensor.matmul_mx(
+                out=acc,
+                lhsT=lhs[0][:, lhs_cols].bitcast(FP8X4),
+                lhsT_scale=lhs[1][:, lhs_cols],
+                rhs=rhs[0][:, rhs_cols].bitcast(FP8X4),
+                rhs_scale=rhs[1][:, rhs_cols],
+                start=start,
+                stop=stop,
+            )
+
+        def operand(name):
+            return sbuf([P, S], U32, name + "_codes"), sbuf([P, S], U8, name + "_scales")
+
+        def interleave_on_scalar(dst, src):
+            nc.scalar.copy(
+                out=dst.rearrange("p (c i t) -> p c t i", i=4, t=PACK),
+                in_=src.rearrange("p t (c i) -> p c t i", i=4),
+            )
+
+        xs_win = sbuf([P, T], U8, "xs_win", tag="raw_c")
+        nc.vector.memset(xs_win[:].bitcast(I32), 0)
+        for q in range(4):
+            nc.sync.dma_start(
+                out=xs_win[32 * q : 32 * q + 4, :].bitcast(I32),
+                in_=x_scales[0, 4 * q : 4 * q + 4, :].bitcast(I32),
+            )
+        offs_t = lists.tile([P, S // 16], U16, name="offs_t")
+        nc.sync.dma_start(offs_t[:], offs)
+        w1_raw = sbuf([P, PACK, H], F32, "w1_raw", tag="raw_a")
+        nc.sync.dma_start(out=w1_raw[:], in_=w1.rearrange("(p j) c -> p j c", j=PACK))
+        p1_t = lists.tile([P, S // 16], U16, name="p1_t")
+        nc.sync.dma_start(p1_t[:], p1)
+        p2_t = lists.tile([P, S // 16], U16, name="p2_t")
+        nc.sync.dma_start(p2_t[:], p2)
+        xw_win = sbuf([P, T], U32, "xw_win", tag="raw_b")
+        nc.sync.dma_start(
+            out=xw_win[:].bitcast(I32),
+            in_=x_words[0].rearrange("p n t -> p (n t)").bitcast(I32),
+        )
+
+        ident = sbuf([P, P], F32, "ident")
+        make_identity(nc, ident[:])
+
+        x_q = operand("x")
+        nc.vector.tensor_copy(x_q[1][:], xs_win[:].indirect(offs_t[:]))
+
+        w1_q = operand("w1")
+        w1_view = w1_raw[:].rearrange("p j (m t) -> p m t j", t=PACK)
+        w1_bf = [sbuf([P, 2 * P * PACK], BF16, "w1_bf%d" % u) for u in range(2)]
+        w1_bf_view = [b[:].rearrange("p (t m j) -> p m t j", t=2, j=PACK) for b in w1_bf]
+        nc.vector.tensor_copy(out=w1_bf_view[0], in_=w1_view[:, :, 0:2, :])
+        nc.scalar.activation(out=w1_bf_view[1], in_=w1_view[:, :, 2:4, :], func=COPY)
+        for u in range(2):
+            c = slice(2 * P * u, 2 * P * (u + 1))
+            quantize(w1_q[0][:, c], w1_q[1][:, c], w1_bf[u][:])
+
+        for lo in (0, HALF):
+            nc.vector.tensor_copy(
+                x_q[0][:, lo : lo + HALF], xw_win[:].indirect(cols(offs_t, lo, lo + HALF))
+            )
+
+        ga_t = sbuf([P, S], F32, "ga_t", tag="w1_bf0")
+        nc.sync.dma_start(out=ga_t[:], in_=ga)
+        gb_t = sbuf([P, S], F32, "gb_t", tag="w1_bf1")
+        nc.sync.dma_start(out=gb_t[:], in_=gb)
+
+        w_raw = []
+        for name, w, tag in (("w2", w2, "raw_a"), ("w3", w3, "raw_c"), ("w4", w4, "raw_b")):
+            raw = sbuf([P, PACK, N], F32, name + "_raw", tag=tag)
+            nc.sync.dma_start(out=raw[:], in_=w.rearrange("(p j) c -> p j c", j=PACK))
+            w_raw.append(raw)
+
+        y_win = [sbuf([P, S], F32, "y_win%d" % t) for t in range(PACK)]
+        y_all = sbuf([P, PACK, S], F32, "y_all")
+        for t in range(PACK):
+            acc = bank([P, S], "y_acc%d" % t, "o%d" % t)
+            plane = slice(P * t, P * (t + 1))
+            if t == 0:
+                for lo in (0, HALF):
+                    c = slice(lo, lo + HALF)
+                    matmul_mx(acc[:, c], w1_q, plane, x_q, c, True, True)
+            else:
+                matmul_mx(acc[:], w1_q, plane, x_q, slice(0, S), True, True)
+            nc.scalar.copy(out=y_win[t][:], in_=acc[:])
+            nc.sync.dma_start(out=y_all[:, t, :], in_=y_win[t][:])
+
+        if len(PE_PLANES) < PACK:
+            gb_z = sbuf([P, S], F32, "gb_z")
+            nc.vector.tensor_scalar(gb_z[:], gb_t[:], -2.0, None, MULT)
+
+        def gather(dst, window, places, gate, lo, hi):
+            nc.vector.tensor_tensor(
+                dst, window[:].indirect(cols(places, lo, hi)), gate[:, lo:hi], MULT
+            )
+
+        h_win = [sbuf([P, S], F32, "h_win%d" % t) for t in range(PACK)]
+        h_all = sbuf([P, PACK, S], F32, "h_all")
+        first = [sbuf([P, S], F32, "first%d" % t) for t in range(PACK)]
+        second = [sbuf([P, S], F32, "second%d" % t) for t in range(PACK)]
+
+        def add_h(t):
+            if t in PE_PLANES:
+                turned = bank([P, S], "h_turned%d" % t, "zt", bufs=2)
+                for b in range(S // P):
+                    c = slice(P * b, P * (b + 1))
+                    for i, term in enumerate((first[t], second[t])):
+                        nc.tensor.matmul(
+                            turned[:, c], lhsT=term[:, c], rhs=ident[:],
+                            start=(i == 0), stop=(i == 1), is_transpose=True,
+                        )
+                rows = sbuf([P, S], F32, "h_rows%d" % t)
+                nc.scalar.activation(out=rows[:], in_=turned[:], func=COPY, scale=-2.0)
+                back = bank([P, S], "h_back%d" % t, ("words", "o_mid")[t % 2])
+                for b in range(S // P):
+                    c = slice(P * b, P * (b + 1))
+                    nc.tensor.transpose(back[:, c], rows[:, c], ident[:])
+                nc.scalar.copy(out=h_win[t][:], in_=back[:])
+            else:
+                nc.vector.scalar_tensor_tensor(
+                    h_win[t][:], first[t][:], -2.0, second[t][:], MULT, ADD
+                )
+            nc.sync.dma_start(out=h_all[:, t, :], in_=h_win[t][:])
+
+        for t in range(PACK):
+            for lo in (0, HALF):
+                gather(first[t][:, lo : lo + HALF], y_win[t], p1_t, ga_t, lo, lo + HALF)
+            if t > 0:
+                add_h(t - 1)
+            gate = gb_t if t in PE_PLANES else gb_z
+            for lo in (0, HALF):
+                gather(second[t][:, lo : lo + HALF], y_win[t], p2_t, gate, lo, lo + HALF)
+        add_h(PACK - 1)
+
+        def weight(i, tag):
+            bf = sbuf([P, N * PACK], BF16, "w_bf%d" % i, tag=tag)
+            interleave_on_scalar(bf[:], w_raw[i][:])
+            q = operand("w%d" % (i + 2))
+            quantize(q[0][:], q[1][:], bf[:])
+            return q
+
+        w2_q = weight(0, "w2_bf")
+        y_bf = sbuf([P, S * PACK], BF16, "y_bf")
+        interleave_on_scalar(y_bf[:], y_all[:])
+        y_q = operand("y")
+        quantize(y_q[0][:], y_q[1][:], y_bf[:])
+        w3_q = weight(1, "hold_d0")
+        w4_q = weight(2, "hold_c0")
+
+        h_q = operand("h")
+        z_q = operand("z")
+
+        def quantize_h(half, tag):
+            lo = half * HALF
+            bf = sbuf([P, HALF * PACK], BF16, "h_bf%d" % half, tag=tag)
+            nc.scalar.activation(
+                out=bf[:].rearrange("p (c i t) -> p c t i", i=4, t=PACK),
+                in_=h_all[:, :, lo : lo + HALF].rearrange("p t (c i) -> p c t i", i=4),
+                func=COPY,
+                scale=-0.5,
+            )
+            quantize(h_q[0][:, lo : lo + HALF], h_q[1][:, lo : lo + HALF], bf[:])
+
+        for s, (lo, hi) in enumerate(Z_SLICES):
+            width = hi - lo
+            blocks = width // P
+            c_t = sbuf([P, PACK, width], F32, "c%d" % s, tag="hold_c%d" % s)
+            c_planes = [c_t[:, t, :] for t in range(PACK)]
+            last = s == len(Z_SLICES) - 1
+            d_t = sbuf([P, PACK, width], F32, "d%d" % s, tag="hold_d%d" % s)
+            if last:
+                for t in range(PACK):
+                    gather(d_t[:, t, :], h_win[t], p2_t, gb_t, lo, hi)
+                gather(c_planes[0], h_win[0], p1_t, ga_t, lo, hi)
+                partial = sbuf([P, PACK, width], F32, "partial", tag="hold_partial")
+                nc.vector.scalar_tensor_tensor(
+                    partial[:], d_t[:], -1.0, y_all[:, :, lo:hi], MULT, SUBTRACT
+                )
+                for t in range(1, PACK):
+                    gather(c_planes[t], h_win[t], p1_t, ga_t, lo, hi)
+                z_bf = sbuf([P, width * PACK], BF16, "z_bf%d" % s)
+                nc.vector.tensor_tensor(
+                    z_bf[:].rearrange("p (c i t) -> p c t i", i=4, t=PACK),
+                    partial[:].rearrange("p t (c i) -> p c t i", i=4),
+                    c_t[:].rearrange("p t (c i) -> p c t i", i=4),
+                    SUBTRACT,
+                )
+            else:
+                z_rows = sbuf([P, blocks, 2, 2 * P], BF16, "z_rows%d" % s)
+                words = bank([P, blocks, 2, P], "words%d" % s, "words")
+                for u in range(2):
+                    zt = bank([P, blocks, 2, P], "zt%d_%d" % (s, u), "zt", bufs=2)
+                    for e in range(2):
+                        t = 2 * u + e
+                        gather(d_t[:, t, :], h_win[t], p2_t, gb_t, lo, hi)
+                        gather(c_planes[t], h_win[t], p1_t, ga_t, lo, hi)
+                        for b in range(blocks):
+                            terms = (
+                                y_win[t][:, lo + P * b : lo + P * (b + 1)],
+                                d_t[:, t, P * b : P * (b + 1)],
+                                c_planes[t][:, P * b : P * (b + 1)],
+                            )
+                            for i, term in enumerate(terms):
+                                nc.tensor.matmul(
+                                    zt[:, b, e, :], lhsT=term, rhs=ident[:],
+                                    start=(i == 0), stop=(i == 2), is_transpose=True,
+                                )
+                    nc.scalar.activation(
+                        out=z_rows[:, :, u, :].rearrange("j b (p e) -> j b p e", e=2),
+                        in_=zt[:].rearrange("j b e p -> j b p e"),
+                        func=COPY,
+                        scale=-1.0,
+                    )
+                    for b in range(blocks):
+                        nc.tensor.transpose(
+                            words[:, b, u, :], z_rows[:, b, u, :].bitcast(F32), ident[:]
+                        )
+                if s == 0:
+                    quantize_h(0, "hold_c1")
+                    quantize_h(1, "hold_d2")
+                z_tag = ("hold_c2", "hold_partial")[s]
+                z_bf = sbuf([P, width * PACK], BF16, "z_bf%d" % s, tag=z_tag)
+                nc.scalar.copy(
+                    out=z_bf[:].bitcast(F32).rearrange("p (b j u) -> p b j u", b=blocks, u=2),
+                    in_=words[:].rearrange("p b u j -> p b j u"),
+                )
+            c = slice(lo, hi)
+            quantize(z_q[0][:, c], z_q[1][:, c], z_bf[:])
+
+            result = sbuf([P, N // P, width], F32, "result%d" % s)
+            pairs = ((w2_q, y_q), (w3_q, h_q), (w4_q, z_q))
+            if s == 1:
+                acc = bank([P, N // P, width], "o_mid", "o_mid")
+                for m in range(N // P):
+                    for i, (w_q, v_q) in enumerate(pairs):
+                        matmul_mx(
+                            acc[:, m, :], w_q, slice(P * m, P * (m + 1)), v_q, c, i == 0, i == 2
+                        )
+                nc.scalar.copy(out=result[:], in_=acc[:])
+            else:
+                accs = [bank([P, S], "o_acc%d_%d" % (s, m), "o%d" % m) for m in range(N // P)]
+                for i, (w_q, v_q) in enumerate(pairs):
+                    for m in range(N // P):
+                        matmul_mx(
+                            accs[m][:, :width], w_q, slice(P * m, P * (m + 1)), v_q, c,
+                            i == 0, i == 2,
+                        )
+                for m in range(N // P):
+                    if last and m % 2 == 1:
+                        nc.vector.tensor_copy(out=result[:, m, :], in_=accs[m][:, :width])
+                    else:
+                        nc.scalar.copy(out=result[:, m, :], in_=accs[m][:, :width])
+            nc.sync.dma_start(
+                out=out.rearrange("(m p) j -> p m j", p=P)[:, :, c], in_=result[:]
+            )

@@ -20,7 +20,7 @@ COPY = mybir.ActivationFunctionType.Copy
 P = 128
 PACK = 4
 HALF = S // 2
-PE_PLANES = (0, 1, 2, 3)
+PE_PLANES = ()
 SUBTRACT = mybir.AluOpType.subtract
 Z_SLICES = ((0, 256), (256, 384), (384, 512))
 
@@ -119,7 +119,9 @@ def tile_picked_cheb3_none_p_kernel(
             nc.sync.dma_start(out=raw[:], in_=w.rearrange("(p j) c -> p j c", j=PACK))
             w_raw.append(raw)
 
-        y_win = [sbuf([P, S], F32, "y_win%d" % t) for t in range(PACK)]
+        y_win = [sbuf([P, 2 * S], F32, "y_win%d" % t) for t in range(PACK)]
+        for t in range(PACK):
+            nc.vector.memset(y_win[t][:, S:], 0.0)
         y_all = sbuf([P, PACK, S], F32, "y_all")
         for t in range(PACK):
             acc = bank([P, S], "y_acc%d" % t, "o%d" % t)
@@ -130,8 +132,8 @@ def tile_picked_cheb3_none_p_kernel(
                     matmul_mx(acc[:, c], w1_q, plane, x_q, c, True, True)
             else:
                 matmul_mx(acc[:], w1_q, plane, x_q, slice(0, S), True, True)
-            nc.scalar.copy(out=y_win[t][:], in_=acc[:])
-            nc.sync.dma_start(out=y_all[:, t, :], in_=y_win[t][:])
+            nc.scalar.copy(out=y_win[t][:, :S], in_=acc[:])
+            nc.sync.dma_start(out=y_all[:, t, :], in_=y_win[t][:, :S])
 
         if len(PE_PLANES) < PACK:
             gb_z = sbuf([P, S], F32, "gb_z")
@@ -171,13 +173,11 @@ def tile_picked_cheb3_none_p_kernel(
             nc.sync.dma_start(out=h_all[:, t, :], in_=h_win[t][:])
 
         for t in range(PACK):
-            for lo in (0, HALF):
-                gather(first[t][:, lo : lo + HALF], y_win[t], p1_t, ga_t, lo, lo + HALF)
+            gather(first[t][:], y_win[t], p1_t, ga_t, 0, S)
             if t > 0:
                 add_h(t - 1)
             gate = gb_t if t in PE_PLANES else gb_z
-            for lo in (0, HALF):
-                gather(second[t][:, lo : lo + HALF], y_win[t], p2_t, gate, lo, lo + HALF)
+            gather(second[t][:], y_win[t], p2_t, gate, 0, S)
         add_h(PACK - 1)
 
         def weight(i, tag):
@@ -212,15 +212,19 @@ def tile_picked_cheb3_none_p_kernel(
         for s, (lo, hi) in enumerate(Z_SLICES):
             width = hi - lo
             blocks = width // P
-            c_t = sbuf([P, PACK, width], F32, "c%d" % s, tag="hold_c%d" % s)
-            c_planes = [c_t[:, t, :] for t in range(PACK)]
             last = s == len(Z_SLICES) - 1
-            d_t = sbuf([P, PACK, width], F32, "d%d" % s, tag="hold_d%d" % s)
-            if last:
+            if s == 0:
+                c_t = sbuf([P, PACK, width], F32, "c%d" % s, tag="hold_c0")
+                d_t = sbuf([P, PACK, width], F32, "d%d" % s, tag="hold_d0")
+            else:
+                both = sbuf([P, 2, PACK, width], F32, "cd%d" % s, tag="hold_cd%d" % s)
+                c_t, d_t = both[:, 0], both[:, 1]
+            c_planes = [c_t[:, t, :] for t in range(PACK)]
+            if s > 0:
                 for t in range(PACK):
                     gather(d_t[:, t, :], h_win[t], p2_t, gb_t, lo, hi)
                 gather(c_planes[0], h_win[0], p1_t, ga_t, lo, hi)
-                partial = sbuf([P, PACK, width], F32, "partial", tag="hold_partial")
+                partial = sbuf([P, PACK, width], F32, "partial%d" % s, tag="hold_partial%d" % s)
                 nc.vector.scalar_tensor_tensor(
                     partial[:], d_t[:], -1.0, y_all[:, :, lo:hi], MULT, SUBTRACT
                 )
@@ -264,9 +268,9 @@ def tile_picked_cheb3_none_p_kernel(
                             words[:, b, u, :], z_rows[:, b, u, :].bitcast(F32), ident[:]
                         )
                 if s == 0:
-                    quantize_h(0, "hold_c1")
-                    quantize_h(1, "hold_d2")
-                z_tag = ("hold_c2", "hold_partial")[s]
+                    quantize_h(0, "hold_cd1")
+                    quantize_h(1, "hold_partial1")
+                z_tag = "hold_cd2"
                 z_bf = sbuf([P, width * PACK], BF16, "z_bf%d" % s, tag=z_tag)
                 nc.scalar.copy(
                     out=z_bf[:].bitcast(F32).rearrange("p (b j u) -> p b j u", b=blocks, u=2),

@@ -20,7 +20,7 @@ COPY = mybir.ActivationFunctionType.Copy
 P = 128
 PACK = 4
 HALF = S // 2
-PE_PLANES = ()
+PE_PLANES = (0, 1, 2)
 SUBTRACT = mybir.AluOpType.subtract
 Z_SLICES = ((0, 256), (256, 384), (384, 512))
 
@@ -62,11 +62,11 @@ def tile_picked_cheb3_none_p_kernel(
 
         def interleave_on_scalar(dst, src):
             nc.scalar.copy(
-                out=dst.rearrange("p (c i t) -> p c t i", i=4, t=PACK),
-                in_=src.rearrange("p t (c i) -> p c t i", i=4),
+                out=dst.rearrange("p (c i t) -> p c t i", i=2, t=PACK),
+                in_=src.rearrange("p t (c i) -> p c t i", i=2),
             )
 
-        xs_win = sbuf([P, T], U8, "xs_win", tag="raw_c")
+        xs_win = sbuf([P, T], U8, "xs_win")
         nc.vector.memset(xs_win[:].bitcast(I32), 0)
         for q in range(4):
             nc.sync.dma_start(
@@ -75,17 +75,27 @@ def tile_picked_cheb3_none_p_kernel(
             )
         offs_t = lists.tile([P, S // 16], U16, name="offs_t")
         nc.sync.dma_start(offs_t[:], offs)
-        w1_raw = sbuf([P, PACK, H], F32, "w1_raw", tag="raw_a")
+        w1_raw = sbuf([P, PACK, H], F32, "w1_raw")
         nc.sync.dma_start(out=w1_raw[:], in_=w1.rearrange("(p j) c -> p j c", j=PACK))
         p1_t = lists.tile([P, S // 16], U16, name="p1_t")
         nc.sync.dma_start(p1_t[:], p1)
         p2_t = lists.tile([P, S // 16], U16, name="p2_t")
         nc.sync.dma_start(p2_t[:], p2)
-        xw_win = sbuf([P, T], U32, "xw_win", tag="raw_b")
+        xw_win = sbuf([P, T], U32, "xw_win")
         nc.sync.dma_start(
             out=xw_win[:].bitcast(I32),
             in_=x_words[0].rearrange("p n t -> p (n t)").bitcast(I32),
         )
+
+        ga_t = sbuf([P, S], F32, "ga_t")
+        nc.sync.dma_start(out=ga_t[:], in_=ga)
+        gb_t = sbuf([P, S], F32, "gb_t")
+        nc.sync.dma_start(out=gb_t[:], in_=gb)
+        w_raw = []
+        for name, w in (("w2", w2), ("w3", w3), ("w4", w4)):
+            raw = sbuf([P, PACK, N], F32, name + "_raw")
+            nc.sync.dma_start(out=raw[:], in_=w.rearrange("(p j) c -> p j c", j=PACK))
+            w_raw.append(raw)
 
         ident = sbuf([P, P], F32, "ident")
         make_identity(nc, ident[:])
@@ -108,17 +118,6 @@ def tile_picked_cheb3_none_p_kernel(
                 x_q[0][:, lo : lo + HALF], xw_win[:].indirect(cols(offs_t, lo, lo + HALF))
             )
 
-        ga_t = sbuf([P, S], F32, "ga_t", tag="w1_bf0")
-        nc.sync.dma_start(out=ga_t[:], in_=ga)
-        gb_t = sbuf([P, S], F32, "gb_t", tag="w1_bf1")
-        nc.sync.dma_start(out=gb_t[:], in_=gb)
-
-        w_raw = []
-        for name, w, tag in (("w2", w2, "raw_a"), ("w3", w3, "raw_c"), ("w4", w4, "raw_b")):
-            raw = sbuf([P, PACK, N], F32, name + "_raw", tag=tag)
-            nc.sync.dma_start(out=raw[:], in_=w.rearrange("(p j) c -> p j c", j=PACK))
-            w_raw.append(raw)
-
         y_win = [sbuf([P, 2 * S], F32, "y_win%d" % t) for t in range(PACK)]
         for t in range(PACK):
             nc.vector.memset(y_win[t][:, S:], 0.0)
@@ -127,12 +126,14 @@ def tile_picked_cheb3_none_p_kernel(
             acc = bank([P, S], "y_acc%d" % t, "o%d" % t)
             plane = slice(P * t, P * (t + 1))
             if t == 0:
-                for lo in (0, HALF):
+                early = bank([P, S], "y_early", "o_mid")
+                for lo, part in ((0, early), (HALF, acc)):
                     c = slice(lo, lo + HALF)
-                    matmul_mx(acc[:, c], w1_q, plane, x_q, c, True, True)
+                    matmul_mx(part[:, c], w1_q, plane, x_q, c, True, True)
+                    nc.scalar.copy(out=y_win[t][:, c], in_=part[:, c])
             else:
                 matmul_mx(acc[:], w1_q, plane, x_q, slice(0, S), True, True)
-            nc.scalar.copy(out=y_win[t][:, :S], in_=acc[:])
+                nc.scalar.copy(out=y_win[t][:, :S], in_=acc[:])
             nc.sync.dma_start(out=y_all[:, t, :], in_=y_win[t][:, :S])
 
         if len(PE_PLANES) < PACK:
@@ -149,6 +150,13 @@ def tile_picked_cheb3_none_p_kernel(
         first = [sbuf([P, S], F32, "first%d" % t) for t in range(PACK)]
         second = [sbuf([P, S], F32, "second%d" % t) for t in range(PACK)]
 
+        def weight(i, tag):
+            bf = sbuf([P, N * PACK], BF16, "w_bf%d" % i, tag=tag)
+            interleave_on_scalar(bf[:], w_raw[i][:])
+            q = operand("w%d" % (i + 2))
+            quantize(q[0][:], q[1][:], bf[:])
+            return q
+
         def add_h(t):
             if t in PE_PLANES:
                 turned = bank([P, S], "h_turned%d" % t, "zt", bufs=2)
@@ -159,7 +167,7 @@ def tile_picked_cheb3_none_p_kernel(
                             turned[:, c], lhsT=term[:, c], rhs=ident[:],
                             start=(i == 0), stop=(i == 1), is_transpose=True,
                         )
-                rows = sbuf([P, S], F32, "h_rows%d" % t)
+                rows = sbuf([P, S], F32, "h_rows%d" % t, tag="w%d_raw" % (t + 2))
                 nc.scalar.activation(out=rows[:], in_=turned[:], func=COPY, scale=-2.0)
                 back = bank([P, S], "h_back%d" % t, ("words", "o_mid")[t % 2])
                 for b in range(S // P):
@@ -172,28 +180,21 @@ def tile_picked_cheb3_none_p_kernel(
                 )
             nc.sync.dma_start(out=h_all[:, t, :], in_=h_win[t][:])
 
+        w_qs = []
         for t in range(PACK):
             gather(first[t][:], y_win[t], p1_t, ga_t, 0, S)
             if t > 0:
+                w_qs.append(weight(t - 1, ("w2_bf", "hold_d0", "hold_c0")[t - 1]))
                 add_h(t - 1)
             gate = gb_t if t in PE_PLANES else gb_z
             gather(second[t][:], y_win[t], p2_t, gate, 0, S)
         add_h(PACK - 1)
+        w2_q, w3_q, w4_q = w_qs
 
-        def weight(i, tag):
-            bf = sbuf([P, N * PACK], BF16, "w_bf%d" % i, tag=tag)
-            interleave_on_scalar(bf[:], w_raw[i][:])
-            q = operand("w%d" % (i + 2))
-            quantize(q[0][:], q[1][:], bf[:])
-            return q
-
-        w2_q = weight(0, "w2_bf")
-        y_bf = sbuf([P, S * PACK], BF16, "y_bf")
+        y_bf = sbuf([P, S * PACK], BF16, "y_bf", tag="w4_raw")
         interleave_on_scalar(y_bf[:], y_all[:])
         y_q = operand("y")
         quantize(y_q[0][:], y_q[1][:], y_bf[:])
-        w3_q = weight(1, "hold_d0")
-        w4_q = weight(2, "hold_c0")
 
         h_q = operand("h")
         z_q = operand("z")
@@ -202,12 +203,15 @@ def tile_picked_cheb3_none_p_kernel(
             lo = half * HALF
             bf = sbuf([P, HALF * PACK], BF16, "h_bf%d" % half, tag=tag)
             nc.scalar.activation(
-                out=bf[:].rearrange("p (c i t) -> p c t i", i=4, t=PACK),
-                in_=h_all[:, :, lo : lo + HALF].rearrange("p t (c i) -> p c t i", i=4),
+                out=bf[:].rearrange("p (c i t) -> p c t i", i=2, t=PACK),
+                in_=h_all[:, :, lo : lo + HALF].rearrange("p t (c i) -> p c t i", i=2),
                 func=COPY,
                 scale=-0.5,
             )
             quantize(h_q[0][:, lo : lo + HALF], h_q[1][:, lo : lo + HALF], bf[:])
+
+        quantize_h(0, "hold_cd1")
+        quantize_h(1, "hold_c1")
 
         for s, (lo, hi) in enumerate(Z_SLICES):
             width = hi - lo
@@ -216,11 +220,14 @@ def tile_picked_cheb3_none_p_kernel(
             if s == 0:
                 c_t = sbuf([P, PACK, width], F32, "c%d" % s, tag="hold_c0")
                 d_t = sbuf([P, PACK, width], F32, "d%d" % s, tag="hold_d0")
+            elif s == 1:
+                c_t = sbuf([P, PACK, width], F32, "c%d" % s, tag="hold_c1")
+                d_t = sbuf([P, PACK, width], F32, "d%d" % s, tag="hold_cd1")
             else:
                 both = sbuf([P, 2, PACK, width], F32, "cd%d" % s, tag="hold_cd%d" % s)
                 c_t, d_t = both[:, 0], both[:, 1]
             c_planes = [c_t[:, t, :] for t in range(PACK)]
-            if s > 0:
+            if last:
                 for t in range(PACK):
                     gather(d_t[:, t, :], h_win[t], p2_t, gb_t, lo, hi)
                 gather(c_planes[0], h_win[0], p1_t, ga_t, lo, hi)
@@ -232,13 +239,13 @@ def tile_picked_cheb3_none_p_kernel(
                     gather(c_planes[t], h_win[t], p1_t, ga_t, lo, hi)
                 z_bf = sbuf([P, width * PACK], BF16, "z_bf%d" % s)
                 nc.vector.tensor_tensor(
-                    z_bf[:].rearrange("p (c i t) -> p c t i", i=4, t=PACK),
-                    partial[:].rearrange("p t (c i) -> p c t i", i=4),
-                    c_t[:].rearrange("p t (c i) -> p c t i", i=4),
+                    z_bf[:].rearrange("p (c i t) -> p c t i", i=2, t=PACK),
+                    partial[:].rearrange("p t (c i) -> p c t i", i=2),
+                    c_t[:].rearrange("p t (c i) -> p c t i", i=2),
                     SUBTRACT,
                 )
             else:
-                z_rows = sbuf([P, blocks, 2, 2 * P], BF16, "z_rows%d" % s)
+                z_rows = sbuf([P, blocks, 2, 2 * P], BF16, "z_rows%d" % s, tag=("h_all", "z_rows1")[s])
                 words = bank([P, blocks, 2, P], "words%d" % s, "words")
                 for u in range(2):
                     zt = bank([P, blocks, 2, P], "zt%d_%d" % (s, u), "zt", bufs=2)
@@ -267,10 +274,7 @@ def tile_picked_cheb3_none_p_kernel(
                         nc.tensor.transpose(
                             words[:, b, u, :], z_rows[:, b, u, :].bitcast(F32), ident[:]
                         )
-                if s == 0:
-                    quantize_h(0, "hold_cd1")
-                    quantize_h(1, "hold_partial1")
-                z_tag = "hold_cd2"
+                z_tag = ("hold_cd2", "hold_partial2")[s]
                 z_bf = sbuf([P, width * PACK], BF16, "z_bf%d" % s, tag=z_tag)
                 nc.scalar.copy(
                     out=z_bf[:].bitcast(F32).rearrange("p (b j u) -> p b j u", b=blocks, u=2),
@@ -302,6 +306,9 @@ def tile_picked_cheb3_none_p_kernel(
                         nc.vector.tensor_copy(out=result[:, m, :], in_=accs[m][:, :width])
                     else:
                         nc.scalar.copy(out=result[:, m, :], in_=accs[m][:, :width])
-            nc.sync.dma_start(
-                out=out.rearrange("(m p) j -> p m j", p=P)[:, :, c], in_=result[:]
-            )
+            out_rows = out.rearrange("(m p) j -> p m j", p=P)
+            if last:
+                nc.sync.dma_start(out=out_rows[:, 0:2, c], in_=result[:, 0:2, :])
+                nc.scalar.dma_start(out=out_rows[:, 2:4, c], in_=result[:, 2:4, :])
+            else:
+                nc.sync.dma_start(out=out_rows[:, :, c], in_=result[:])

@@ -20,7 +20,7 @@ COPY = mybir.ActivationFunctionType.Copy
 P = 128
 PACK = 4
 HALF = S // 2
-PE_PLANES = (0, 1, 2)
+PE_PLANES = (0, 1)
 SUBTRACT = mybir.AluOpType.subtract
 Z_SLICES = ((0, 256), (256, 384), (384, 512))
 
@@ -126,7 +126,7 @@ def tile_picked_cheb3_none_p_kernel(
             acc = bank([P, S], "y_acc%d" % t, "o%d" % t)
             plane = slice(P * t, P * (t + 1))
             if t == 0:
-                early = bank([P, S], "y_early", "o_mid")
+                early = bank([P, S], "y_early", "x0")
                 for lo, part in ((0, early), (HALF, acc)):
                     c = slice(lo, lo + HALF)
                     matmul_mx(part[:, c], w1_q, plane, x_q, c, True, True)
@@ -146,8 +146,8 @@ def tile_picked_cheb3_none_p_kernel(
             )
 
         h_win = [sbuf([P, S], F32, "h_win%d" % t) for t in range(PACK)]
-        h_all = sbuf([P, PACK, S], F32, "h_all")
-        first = [sbuf([P, S], F32, "first%d" % t) for t in range(PACK)]
+        h_half = [sbuf([P, PACK, HALF], F32, "h_half%d" % i) for i in range(2)]
+        first = []
         second = [sbuf([P, S], F32, "second%d" % t) for t in range(PACK)]
 
         def weight(i, tag):
@@ -159,7 +159,7 @@ def tile_picked_cheb3_none_p_kernel(
 
         def add_h(t):
             if t in PE_PLANES:
-                turned = bank([P, S], "h_turned%d" % t, "zt", bufs=2)
+                turned = bank([P, S], "h_turned%d" % t, ("x0", "x2")[t])
                 for b in range(S // P):
                     c = slice(P * b, P * (b + 1))
                     for i, term in enumerate((first[t], second[t])):
@@ -167,9 +167,9 @@ def tile_picked_cheb3_none_p_kernel(
                             turned[:, c], lhsT=term[:, c], rhs=ident[:],
                             start=(i == 0), stop=(i == 1), is_transpose=True,
                         )
-                rows = sbuf([P, S], F32, "h_rows%d" % t, tag="w%d_raw" % (t + 2))
+                rows = sbuf([P, S], F32, "h_rows%d" % t, tag=("rows0", "w2_raw")[t])
                 nc.scalar.activation(out=rows[:], in_=turned[:], func=COPY, scale=-2.0)
-                back = bank([P, S], "h_back%d" % t, ("words", "o_mid")[t % 2])
+                back = bank([P, S], "h_back%d" % t, ("x1", "x3")[t])
                 for b in range(S // P):
                     c = slice(P * b, P * (b + 1))
                     nc.tensor.transpose(back[:, c], rows[:, c], ident[:])
@@ -178,23 +178,29 @@ def tile_picked_cheb3_none_p_kernel(
                 nc.vector.scalar_tensor_tensor(
                     h_win[t][:], first[t][:], -2.0, second[t][:], MULT, ADD
                 )
-            nc.sync.dma_start(out=h_all[:, t, :], in_=h_win[t][:])
+            for i in range(2):
+                queue = nc.scalar if t == 0 else nc.sync
+                queue.dma_start(out=h_half[i][:, t, :], in_=h_win[t][:, HALF * i : HALF * (i + 1)])
 
         w_qs = []
         for t in range(PACK):
+            if 0 < t < PACK - 1:
+                w_qs.append(weight(t - 1, ("w2_bf", "w3_bf")[t - 1]))
+            tag = "first%d" % t
+            first.append(sbuf([P, S], F32, "first%d" % t, tag=tag))
             gather(first[t][:], y_win[t], p1_t, ga_t, 0, S)
             if t > 0:
-                w_qs.append(weight(t - 1, ("w2_bf", "hold_d0", "hold_c0")[t - 1]))
                 add_h(t - 1)
             gate = gb_t if t in PE_PLANES else gb_z
             gather(second[t][:], y_win[t], p2_t, gate, 0, S)
         add_h(PACK - 1)
-        w2_q, w3_q, w4_q = w_qs
-
-        y_bf = sbuf([P, S * PACK], BF16, "y_bf", tag="w4_raw")
+        w2_q, w3_q = w_qs
+        w4_q = weight(2, "w4_bf")
+        y_bf = sbuf([P, S * PACK], BF16, "y_bf", tag="w2_raw")
         interleave_on_scalar(y_bf[:], y_all[:])
         y_q = operand("y")
         quantize(y_q[0][:], y_q[1][:], y_bf[:])
+
 
         h_q = operand("h")
         z_q = operand("z")
@@ -204,34 +210,27 @@ def tile_picked_cheb3_none_p_kernel(
             bf = sbuf([P, HALF * PACK], BF16, "h_bf%d" % half, tag=tag)
             nc.scalar.activation(
                 out=bf[:].rearrange("p (c i t) -> p c t i", i=2, t=PACK),
-                in_=h_all[:, :, lo : lo + HALF].rearrange("p t (c i) -> p c t i", i=2),
+                in_=h_half[half][:].rearrange("p t (c i) -> p c t i", i=2),
                 func=COPY,
                 scale=-0.5,
             )
             quantize(h_q[0][:, lo : lo + HALF], h_q[1][:, lo : lo + HALF], bf[:])
 
-        quantize_h(0, "hold_cd1")
-        quantize_h(1, "hold_c1")
+        quantize_h(0, "h_bf0")
+        quantize_h(1, "h_bf1")
 
         for s, (lo, hi) in enumerate(Z_SLICES):
             width = hi - lo
             blocks = width // P
             last = s == len(Z_SLICES) - 1
-            if s == 0:
-                c_t = sbuf([P, PACK, width], F32, "c%d" % s, tag="hold_c0")
-                d_t = sbuf([P, PACK, width], F32, "d%d" % s, tag="hold_d0")
-            elif s == 1:
-                c_t = sbuf([P, PACK, width], F32, "c%d" % s, tag="hold_c1")
-                d_t = sbuf([P, PACK, width], F32, "d%d" % s, tag="hold_cd1")
-            else:
-                both = sbuf([P, 2, PACK, width], F32, "cd%d" % s, tag="hold_cd%d" % s)
-                c_t, d_t = both[:, 0], both[:, 1]
+            both = sbuf([P, 2, PACK, width], F32, "cd%d" % s, tag=("cd0", "h_half0", "z_bf0")[s])
+            c_t, d_t = both[:, 0], both[:, 1]
             c_planes = [c_t[:, t, :] for t in range(PACK)]
             if last:
                 for t in range(PACK):
                     gather(d_t[:, t, :], h_win[t], p2_t, gb_t, lo, hi)
                 gather(c_planes[0], h_win[0], p1_t, ga_t, lo, hi)
-                partial = sbuf([P, PACK, width], F32, "partial%d" % s, tag="hold_partial%d" % s)
+                partial = sbuf([P, PACK, width], F32, "partial", tag="z_bf1")
                 nc.vector.scalar_tensor_tensor(
                     partial[:], d_t[:], -1.0, y_all[:, :, lo:hi], MULT, SUBTRACT
                 )
@@ -245,10 +244,10 @@ def tile_picked_cheb3_none_p_kernel(
                     SUBTRACT,
                 )
             else:
-                z_rows = sbuf([P, blocks, 2, 2 * P], BF16, "z_rows%d" % s, tag=("h_all", "z_rows1")[s])
-                words = bank([P, blocks, 2, P], "words%d" % s, "words")
-                for u in range(2):
-                    zt = bank([P, blocks, 2, P], "zt%d_%d" % (s, u), "zt", bufs=2)
+                z_rows = sbuf([P, blocks, 2, 2 * P], BF16, "z_rows%d" % s, tag=("h_half1", "z_rows1")[s])
+                words = bank([P, blocks, 2, P], "words%d" % s, "x1")
+                for u in (1, 0):
+                    zt = bank([P, blocks, 2, P], "zt%d_%d" % (s, u), ("x3", "x2")[u])
                     for e in range(2):
                         t = 2 * u + e
                         gather(d_t[:, t, :], h_win[t], p2_t, gb_t, lo, hi)
@@ -274,7 +273,7 @@ def tile_picked_cheb3_none_p_kernel(
                         nc.tensor.transpose(
                             words[:, b, u, :], z_rows[:, b, u, :].bitcast(F32), ident[:]
                         )
-                z_tag = ("hold_cd2", "hold_partial2")[s]
+                z_tag = "z_bf%d" % s
                 z_bf = sbuf([P, width * PACK], BF16, "z_bf%d" % s, tag=z_tag)
                 nc.scalar.copy(
                     out=z_bf[:].bitcast(F32).rearrange("p (b j u) -> p b j u", b=blocks, u=2),
@@ -286,20 +285,20 @@ def tile_picked_cheb3_none_p_kernel(
             result = sbuf([P, N // P, width], F32, "result%d" % s)
             pairs = ((w2_q, y_q), (w3_q, h_q), (w4_q, z_q))
             if s == 1:
-                acc = bank([P, N // P, width], "o_mid", "o_mid")
+                acc = bank([P, N // P, width], "o_mid", "x0")
                 for m in range(N // P):
-                    for i, (w_q, v_q) in enumerate(pairs):
+                    for i, (w_q, v_q) in enumerate(reversed(pairs)):
                         matmul_mx(
                             acc[:, m, :], w_q, slice(P * m, P * (m + 1)), v_q, c, i == 0, i == 2
                         )
                 nc.scalar.copy(out=result[:], in_=acc[:])
             else:
-                accs = [bank([P, S], "o_acc%d_%d" % (s, m), "o%d" % m) for m in range(N // P)]
+                tags = [("o%d" % m, 1) for m in range(N // P)]
+                accs = [bank([P, S], "o_acc%d_%d" % (s, m), *tags[m]) for m in range(N // P)]
                 for i, (w_q, v_q) in enumerate(pairs):
                     for m in range(N // P):
                         matmul_mx(
-                            accs[m][:, :width], w_q, slice(P * m, P * (m + 1)), v_q, c,
-                            i == 0, i == 2,
+                            accs[m][:, :width], w_q, slice(P * m, P * (m + 1)), v_q, c, i == 0, i == 2
                         )
                 for m in range(N // P):
                     if last and m % 2 == 1:

@@ -4,7 +4,7 @@ import concourse.mybir as mybir
 from concourse.masks import make_identity
 
 K, T, S, N, H = 512, 2048, 512, 512, 512
-FLOPS = 4 * 2 * 512 * 512 * 512
+FLOPS = 2 * K * H * S + 3 * 2 * H * N * S
 
 F32 = mybir.dt.float32
 BF16 = mybir.dt.bfloat16
@@ -15,14 +15,16 @@ U8 = mybir.dt.uint8
 FP8X4 = mybir.dt.float8_e4m3fn_x4
 MULT = mybir.AluOpType.mult
 ADD = mybir.AluOpType.add
+SUBTRACT = mybir.AluOpType.subtract
 COPY = mybir.ActivationFunctionType.Copy
 
 P = 128
 PACK = 4
+GROUP = 16
 HALF = S // 2
-PE_PLANES = (0, 1)
-SUBTRACT = mybir.AluOpType.subtract
-Z_SLICES = ((0, 256), (256, 384), (384, 512))
+ROW_BLOCKS = N // P
+TURNED_PLANES = (0, 1)
+WIDE, MIDDLE, LAST = slice(0, 256), slice(256, 384), slice(384, 512)
 
 
 def tile_picked_cheb3_none_p_kernel(
@@ -37,14 +39,23 @@ def tile_picked_cheb3_none_p_kernel(
         def sbuf(shape, dtype, name, tag=None):
             return sb.tile(shape, dtype, name=name, tag=tag or name, align_bytes=64)
 
-        def bank(shape, name, tag, bufs=1):
-            return ps.tile(shape, F32, name=name, tag=tag, bufs=bufs)
+        def bank(shape, name, tag):
+            return ps.tile(shape, F32, name=name, tag=tag, bufs=1)
 
-        def cols(tile, lo, hi):
-            return tile[:, lo // 16 : hi // 16]
+        def entries(list_tile, nodes):
+            return list_tile[:, nodes.start // GROUP : nodes.stop // GROUP]
 
-        def quantize(codes, scales, values):
-            nc.vector.quantize_mx(out=codes.bitcast(FP8X4), scales=scales, in_=values)
+        def block(b, start=0):
+            return slice(start + P * b, start + P * (b + 1))
+
+        def operand(name):
+            return sbuf([P, S], U32, name + "_codes"), sbuf([P, S], U8, name + "_scales")
+
+        def quantize(packed, cols, values):
+            codes, scales = packed
+            nc.vector.quantize_mx(
+                out=codes[:, cols].bitcast(FP8X4), scales=scales[:, cols], in_=values
+            )
 
         def matmul_mx(acc, lhs, lhs_cols, rhs, rhs_cols, start, stop):
             nc.tensor.matmul_mx(
@@ -57,13 +68,22 @@ def tile_picked_cheb3_none_p_kernel(
                 stop=stop,
             )
 
-        def operand(name):
-            return sbuf([P, S], U32, name + "_codes"), sbuf([P, S], U8, name + "_scales")
+        def as_interleaved(tile):
+            return tile.rearrange("p (c i t) -> p c t i", i=2, t=PACK)
 
-        def interleave_on_scalar(dst, src):
-            nc.scalar.copy(
-                out=dst.rearrange("p (c i t) -> p c t i", i=2, t=PACK),
-                in_=src.rearrange("p t (c i) -> p c t i", i=2),
+        def as_planes(tile):
+            return tile.rearrange("p t (c i) -> p c t i", i=2)
+
+        def transposed_sum(acc, terms):
+            for i, term in enumerate(terms):
+                nc.tensor.matmul(
+                    acc, lhsT=term, rhs=ident[:],
+                    start=(i == 0), stop=(i == len(terms) - 1), is_transpose=True,
+                )
+
+        def gather(dst, plane, list_tile, gate, nodes):
+            nc.vector.tensor_tensor(
+                dst, plane[:].indirect(entries(list_tile, nodes)), gate[:, nodes], MULT
             )
 
         xs_win = sbuf([P, T], U8, "xs_win")
@@ -73,33 +93,34 @@ def tile_picked_cheb3_none_p_kernel(
                 out=xs_win[32 * q : 32 * q + 4, :].bitcast(I32),
                 in_=x_scales[0, 4 * q : 4 * q + 4, :].bitcast(I32),
             )
-        offs_t = lists.tile([P, S // 16], U16, name="offs_t")
+        offs_t = lists.tile([P, S // GROUP], U16, name="offs_t")
         nc.sync.dma_start(offs_t[:], offs)
         w1_raw = sbuf([P, PACK, H], F32, "w1_raw")
         nc.sync.dma_start(out=w1_raw[:], in_=w1.rearrange("(p j) c -> p j c", j=PACK))
-        p1_t = lists.tile([P, S // 16], U16, name="p1_t")
+        p1_t = lists.tile([P, S // GROUP], U16, name="p1_t")
         nc.sync.dma_start(p1_t[:], p1)
-        p2_t = lists.tile([P, S // 16], U16, name="p2_t")
+        p2_t = lists.tile([P, S // GROUP], U16, name="p2_t")
         nc.sync.dma_start(p2_t[:], p2)
         xw_win = sbuf([P, T], U32, "xw_win")
         nc.sync.dma_start(
             out=xw_win[:].bitcast(I32),
             in_=x_words[0].rearrange("p n t -> p (n t)").bitcast(I32),
         )
-
         ga_t = sbuf([P, S], F32, "ga_t")
         nc.sync.dma_start(out=ga_t[:], in_=ga)
         gb_t = sbuf([P, S], F32, "gb_t")
         nc.sync.dma_start(out=gb_t[:], in_=gb)
-        w_raw = []
+        w_raw = {}
         for name, w in (("w2", w2), ("w3", w3), ("w4", w4)):
             raw = sbuf([P, PACK, N], F32, name + "_raw")
             nc.sync.dma_start(out=raw[:], in_=w.rearrange("(p j) c -> p j c", j=PACK))
-            w_raw.append(raw)
+            w_raw.setdefault(name, raw)
 
         ident = sbuf([P, P], F32, "ident")
         make_identity(nc, ident[:])
 
+        all_nodes = slice(0, S)
+        halves = (slice(0, HALF), slice(HALF, S))
         x_q = operand("x")
         nc.vector.tensor_copy(x_q[1][:], xs_win[:].indirect(offs_t[:]))
 
@@ -110,13 +131,10 @@ def tile_picked_cheb3_none_p_kernel(
         nc.vector.tensor_copy(out=w1_bf_view[0], in_=w1_view[:, :, 0:2, :])
         nc.scalar.activation(out=w1_bf_view[1], in_=w1_view[:, :, 2:4, :], func=COPY)
         for u in range(2):
-            c = slice(2 * P * u, 2 * P * (u + 1))
-            quantize(w1_q[0][:, c], w1_q[1][:, c], w1_bf[u][:])
+            quantize(w1_q, slice(2 * P * u, 2 * P * (u + 1)), w1_bf[u][:])
 
-        for lo in (0, HALF):
-            nc.vector.tensor_copy(
-                x_q[0][:, lo : lo + HALF], xw_win[:].indirect(cols(offs_t, lo, lo + HALF))
-            )
+        for nodes in halves:
+            nc.vector.tensor_copy(x_q[0][:, nodes], xw_win[:].indirect(entries(offs_t, nodes)))
 
         y_win = [sbuf([P, 2 * S], F32, "y_win%d" % t) for t in range(PACK)]
         for t in range(PACK):
@@ -124,190 +142,191 @@ def tile_picked_cheb3_none_p_kernel(
         y_all = sbuf([P, PACK, S], F32, "y_all")
         for t in range(PACK):
             acc = bank([P, S], "y_acc%d" % t, "o%d" % t)
-            plane = slice(P * t, P * (t + 1))
             if t == 0:
                 early = bank([P, S], "y_early", "x0")
-                for lo, part in ((0, early), (HALF, acc)):
-                    c = slice(lo, lo + HALF)
-                    matmul_mx(part[:, c], w1_q, plane, x_q, c, True, True)
-                    nc.scalar.copy(out=y_win[t][:, c], in_=part[:, c])
+                pieces = ((halves[0], early), (halves[1], acc))
             else:
-                matmul_mx(acc[:], w1_q, plane, x_q, slice(0, S), True, True)
-                nc.scalar.copy(out=y_win[t][:, :S], in_=acc[:])
-            nc.sync.dma_start(out=y_all[:, t, :], in_=y_win[t][:, :S])
+                pieces = ((all_nodes, acc),)
+            for nodes, piece in pieces:
+                matmul_mx(piece[:, nodes], w1_q, block(t), x_q, nodes, True, True)
+                nc.scalar.copy(out=y_win[t][:, nodes], in_=piece[:, nodes])
+            nc.sync.dma_start(out=y_all[:, t, :], in_=y_win[t][:, all_nodes])
 
-        if len(PE_PLANES) < PACK:
-            gb_z = sbuf([P, S], F32, "gb_z")
-            nc.vector.tensor_scalar(gb_z[:], gb_t[:], -2.0, None, MULT)
-
-        def gather(dst, window, places, gate, lo, hi):
-            nc.vector.tensor_tensor(
-                dst, window[:].indirect(cols(places, lo, hi)), gate[:, lo:hi], MULT
-            )
+        gb_scaled = sbuf([P, S], F32, "gb_z")
+        nc.vector.tensor_scalar(gb_scaled[:], gb_t[:], -2.0, None, MULT)
 
         h_win = [sbuf([P, S], F32, "h_win%d" % t) for t in range(PACK)]
         h_half = [sbuf([P, PACK, HALF], F32, "h_half%d" % i) for i in range(2)]
         first = []
         second = [sbuf([P, S], F32, "second%d" % t) for t in range(PACK)]
 
-        def weight(i, tag):
-            bf = sbuf([P, N * PACK], BF16, "w_bf%d" % i, tag=tag)
-            interleave_on_scalar(bf[:], w_raw[i][:])
-            q = operand("w%d" % (i + 2))
-            quantize(q[0][:], q[1][:], bf[:])
-            return q
+        def weight(name, number):
+            values = sbuf([P, N * PACK], BF16, "w_bf%d" % number, tag=name + "_bf")
+            nc.scalar.copy(out=as_interleaved(values[:]), in_=as_planes(w_raw[name][:]))
+            packed = operand(name)
+            quantize(packed, slice(0, N), values[:])
+            return packed
 
         def add_h(t):
-            if t in PE_PLANES:
-                turned = bank([P, S], "h_turned%d" % t, ("x0", "x2")[t])
+            if t in TURNED_PLANES:
+                turned = bank([P, S], "h_turned%d" % t, "x%d" % (2 * t))
                 for b in range(S // P):
-                    c = slice(P * b, P * (b + 1))
-                    for i, term in enumerate((first[t], second[t])):
-                        nc.tensor.matmul(
-                            turned[:, c], lhsT=term[:, c], rhs=ident[:],
-                            start=(i == 0), stop=(i == 1), is_transpose=True,
-                        )
+                    cols = block(b)
+                    transposed_sum(turned[:, cols], (first[t][:, cols], second[t][:, cols]))
                 rows = sbuf([P, S], F32, "h_rows%d" % t, tag=("rows0", "w2_raw")[t])
                 nc.scalar.activation(out=rows[:], in_=turned[:], func=COPY, scale=-2.0)
-                back = bank([P, S], "h_back%d" % t, ("x1", "x3")[t])
+                back = bank([P, S], "h_back%d" % t, "x%d" % (2 * t + 1))
                 for b in range(S // P):
-                    c = slice(P * b, P * (b + 1))
-                    nc.tensor.transpose(back[:, c], rows[:, c], ident[:])
+                    nc.tensor.transpose(back[:, block(b)], rows[:, block(b)], ident[:])
                 nc.scalar.copy(out=h_win[t][:], in_=back[:])
             else:
                 nc.vector.scalar_tensor_tensor(
                     h_win[t][:], first[t][:], -2.0, second[t][:], MULT, ADD
                 )
+            queue = nc.scalar if t == 0 else nc.sync
             for i in range(2):
-                queue = nc.scalar if t == 0 else nc.sync
-                queue.dma_start(out=h_half[i][:, t, :], in_=h_win[t][:, HALF * i : HALF * (i + 1)])
+                queue.dma_start(out=h_half[i][:, t, :], in_=h_win[t][:, halves[i]])
 
-        w_qs = []
-        for t in range(PACK):
-            if 0 < t < PACK - 1:
-                w_qs.append(weight(t - 1, ("w2_bf", "w3_bf")[t - 1]))
-            tag = "first%d" % t
-            first.append(sbuf([P, S], F32, "first%d" % t, tag=tag))
-            gather(first[t][:], y_win[t], p1_t, ga_t, 0, S)
+        def gather_y(t):
+            first.append(sbuf([P, S], F32, "first%d" % t))
+            gather(first[t][:], y_win[t], p1_t, ga_t, all_nodes)
             if t > 0:
                 add_h(t - 1)
-            gate = gb_t if t in PE_PLANES else gb_z
-            gather(second[t][:], y_win[t], p2_t, gate, 0, S)
-        add_h(PACK - 1)
-        w2_q, w3_q = w_qs
-        w4_q = weight(2, "w4_bf")
-        y_bf = sbuf([P, S * PACK], BF16, "y_bf", tag="w2_raw")
-        interleave_on_scalar(y_bf[:], y_all[:])
-        y_q = operand("y")
-        quantize(y_q[0][:], y_q[1][:], y_bf[:])
+            gate = gb_t if t in TURNED_PLANES else gb_scaled
+            gather(second[t][:], y_win[t], p2_t, gate, all_nodes)
 
+        gather_y(0)
+        w2_q = weight("w2", 0)
+        gather_y(1)
+        w3_q = weight("w3", 1)
+        gather_y(2)
+        gather_y(3)
+        add_h(3)
+        w4_q = weight("w4", 2)
+
+        y_bf = sbuf([P, S * PACK], BF16, "y_bf", tag="w2_raw")
+        nc.scalar.copy(out=as_interleaved(y_bf[:]), in_=as_planes(y_all[:]))
+        y_q = operand("y")
+        quantize(y_q, all_nodes, y_bf[:])
 
         h_q = operand("h")
         z_q = operand("z")
-
-        def quantize_h(half, tag):
-            lo = half * HALF
-            bf = sbuf([P, HALF * PACK], BF16, "h_bf%d" % half, tag=tag)
+        for i in range(2):
+            h_bf = sbuf([P, HALF * PACK], BF16, "h_bf%d" % i)
             nc.scalar.activation(
-                out=bf[:].rearrange("p (c i t) -> p c t i", i=2, t=PACK),
-                in_=h_half[half][:].rearrange("p t (c i) -> p c t i", i=2),
-                func=COPY,
-                scale=-0.5,
+                out=as_interleaved(h_bf[:]), in_=as_planes(h_half[i][:]), func=COPY, scale=-0.5
             )
-            quantize(h_q[0][:, lo : lo + HALF], h_q[1][:, lo : lo + HALF], bf[:])
+            quantize(h_q, halves[i], h_bf[:])
 
-        quantize_h(0, "h_bf0")
-        quantize_h(1, "h_bf1")
+        def terms_of_z(number, nodes, tag):
+            both = sbuf([P, 2, PACK, nodes.stop - nodes.start], F32, "cd%d" % number, tag=tag)
+            return both[:, 0], both[:, 1]
 
-        for s, (lo, hi) in enumerate(Z_SLICES):
-            width = hi - lo
-            blocks = width // P
-            last = s == len(Z_SLICES) - 1
-            both = sbuf([P, 2, PACK, width], F32, "cd%d" % s, tag=("cd0", "h_half0", "z_bf0")[s])
-            c_t, d_t = both[:, 0], both[:, 1]
-            c_planes = [c_t[:, t, :] for t in range(PACK)]
-            if last:
-                for t in range(PACK):
-                    gather(d_t[:, t, :], h_win[t], p2_t, gb_t, lo, hi)
-                gather(c_planes[0], h_win[0], p1_t, ga_t, lo, hi)
-                partial = sbuf([P, PACK, width], F32, "partial", tag="z_bf1")
-                nc.vector.scalar_tensor_tensor(
-                    partial[:], d_t[:], -1.0, y_all[:, :, lo:hi], MULT, SUBTRACT
-                )
-                for t in range(1, PACK):
-                    gather(c_planes[t], h_win[t], p1_t, ga_t, lo, hi)
-                z_bf = sbuf([P, width * PACK], BF16, "z_bf%d" % s)
-                nc.vector.tensor_tensor(
-                    z_bf[:].rearrange("p (c i t) -> p c t i", i=2, t=PACK),
-                    partial[:].rearrange("p t (c i) -> p c t i", i=2),
-                    c_t[:].rearrange("p t (c i) -> p c t i", i=2),
-                    SUBTRACT,
-                )
-            else:
-                z_rows = sbuf([P, blocks, 2, 2 * P], BF16, "z_rows%d" % s, tag=("h_half1", "z_rows1")[s])
-                words = bank([P, blocks, 2, P], "words%d" % s, "x1")
-                for u in (1, 0):
-                    zt = bank([P, blocks, 2, P], "zt%d_%d" % (s, u), ("x3", "x2")[u])
-                    for e in range(2):
-                        t = 2 * u + e
-                        gather(d_t[:, t, :], h_win[t], p2_t, gb_t, lo, hi)
-                        gather(c_planes[t], h_win[t], p1_t, ga_t, lo, hi)
-                        for b in range(blocks):
-                            terms = (
-                                y_win[t][:, lo + P * b : lo + P * (b + 1)],
-                                d_t[:, t, P * b : P * (b + 1)],
-                                c_planes[t][:, P * b : P * (b + 1)],
-                            )
-                            for i, term in enumerate(terms):
-                                nc.tensor.matmul(
-                                    zt[:, b, e, :], lhsT=term, rhs=ident[:],
-                                    start=(i == 0), stop=(i == 2), is_transpose=True,
-                                )
-                    nc.scalar.activation(
-                        out=z_rows[:, :, u, :].rearrange("j b (p e) -> j b p e", e=2),
-                        in_=zt[:].rearrange("j b e p -> j b p e"),
-                        func=COPY,
-                        scale=-1.0,
-                    )
+        def z_by_transposes(number, nodes, terms_tag, rows_tag):
+            blocks = (nodes.stop - nodes.start) // P
+            by_p1, by_p2 = terms_of_z(number, nodes, terms_tag)
+            z_rows = sbuf([P, blocks, 2, 2 * P], BF16, "z_rows%d" % number, tag=rows_tag)
+            words = bank([P, blocks, 2, P], "words%d" % number, "x1")
+            for u in (1, 0):
+                minus_z = bank([P, blocks, 2, P], "zt%d_%d" % (number, u), "x%d" % (3 - u))
+                for e in range(2):
+                    t = 2 * u + e
+                    gather(by_p2[:, t, :], h_win[t], p2_t, gb_t, nodes)
+                    gather(by_p1[:, t, :], h_win[t], p1_t, ga_t, nodes)
                     for b in range(blocks):
-                        nc.tensor.transpose(
-                            words[:, b, u, :], z_rows[:, b, u, :].bitcast(F32), ident[:]
+                        transposed_sum(
+                            minus_z[:, b, e, :],
+                            (
+                                y_win[t][:, block(b, nodes.start)],
+                                by_p2[:, t, block(b)],
+                                by_p1[:, t, block(b)],
+                            ),
                         )
-                z_tag = "z_bf%d" % s
-                z_bf = sbuf([P, width * PACK], BF16, "z_bf%d" % s, tag=z_tag)
-                nc.scalar.copy(
-                    out=z_bf[:].bitcast(F32).rearrange("p (b j u) -> p b j u", b=blocks, u=2),
-                    in_=words[:].rearrange("p b u j -> p b j u"),
+                nc.scalar.activation(
+                    out=z_rows[:, :, u, :].rearrange("j b (p e) -> j b p e", e=2),
+                    in_=minus_z[:].rearrange("j b e p -> j b p e"),
+                    func=COPY,
+                    scale=-1.0,
                 )
-            c = slice(lo, hi)
-            quantize(z_q[0][:, c], z_q[1][:, c], z_bf[:])
+                for b in range(blocks):
+                    nc.tensor.transpose(
+                        words[:, b, u, :], z_rows[:, b, u, :].bitcast(F32), ident[:]
+                    )
+            z_bf = sbuf([P, blocks * P * PACK], BF16, "z_bf%d" % number)
+            nc.scalar.copy(
+                out=z_bf[:].bitcast(F32).rearrange("p (b j u) -> p b j u", b=blocks, u=2),
+                in_=words[:].rearrange("p b u j -> p b j u"),
+            )
+            return z_bf
 
-            result = sbuf([P, N // P, width], F32, "result%d" % s)
-            pairs = ((w2_q, y_q), (w3_q, h_q), (w4_q, z_q))
-            if s == 1:
-                acc = bank([P, N // P, width], "o_mid", "x0")
-                for m in range(N // P):
-                    for i, (w_q, v_q) in enumerate(reversed(pairs)):
-                        matmul_mx(
-                            acc[:, m, :], w_q, slice(P * m, P * (m + 1)), v_q, c, i == 0, i == 2
-                        )
-                nc.scalar.copy(out=result[:], in_=acc[:])
-            else:
-                tags = [("o%d" % m, 1) for m in range(N // P)]
-                accs = [bank([P, S], "o_acc%d_%d" % (s, m), *tags[m]) for m in range(N // P)]
-                for i, (w_q, v_q) in enumerate(pairs):
-                    for m in range(N // P):
-                        matmul_mx(
-                            accs[m][:, :width], w_q, slice(P * m, P * (m + 1)), v_q, c, i == 0, i == 2
-                        )
-                for m in range(N // P):
-                    if last and m % 2 == 1:
-                        nc.vector.tensor_copy(out=result[:, m, :], in_=accs[m][:, :width])
-                    else:
-                        nc.scalar.copy(out=result[:, m, :], in_=accs[m][:, :width])
-            out_rows = out.rearrange("(m p) j -> p m j", p=P)
-            if last:
-                nc.sync.dma_start(out=out_rows[:, 0:2, c], in_=result[:, 0:2, :])
-                nc.scalar.dma_start(out=out_rows[:, 2:4, c], in_=result[:, 2:4, :])
-            else:
-                nc.sync.dma_start(out=out_rows[:, :, c], in_=result[:])
+        def z_on_vector(number, nodes, terms_tag, z_tag):
+            width = nodes.stop - nodes.start
+            by_p1, by_p2 = terms_of_z(number, nodes, terms_tag)
+            for t in range(PACK):
+                gather(by_p2[:, t, :], h_win[t], p2_t, gb_t, nodes)
+            gather(by_p1[:, 0, :], h_win[0], p1_t, ga_t, nodes)
+            partial = sbuf([P, PACK, width], F32, "partial")
+            nc.vector.scalar_tensor_tensor(
+                partial[:], by_p2, -1.0, y_all[:, :, nodes], MULT, SUBTRACT
+            )
+            for t in range(1, PACK):
+                gather(by_p1[:, t, :], h_win[t], p1_t, ga_t, nodes)
+            z_bf = sbuf([P, width * PACK], BF16, "z_bf%d" % number, tag=z_tag)
+            nc.vector.tensor_tensor(
+                as_interleaved(z_bf[:]), as_planes(partial[:]), as_planes(by_p1), SUBTRACT
+            )
+            return z_bf
+
+        with_y, with_h, with_z = (w2_q, y_q), (w3_q, h_q), (w4_q, z_q)
+        out_rows = out.rearrange("(m p) j -> p m j", p=P)
+
+        def products_in_four_banks(number, nodes, passes):
+            width = nodes.stop - nodes.start
+            accs = [
+                bank([P, S], "o_acc%d_%d" % (number, m), "o%d" % m)[:, :width]
+                for m in range(ROW_BLOCKS)
+            ]
+            for i, (w_q, v_q) in enumerate(passes):
+                for m in range(ROW_BLOCKS):
+                    matmul_mx(accs[m], w_q, block(m), v_q, nodes, i == 0, i == len(passes) - 1)
+            return accs
+
+        def output_wide():
+            result = sbuf([P, ROW_BLOCKS, WIDE.stop - WIDE.start], F32, "result0")
+            accs = products_in_four_banks(0, WIDE, (with_y, with_z, with_h))
+            for m in range(ROW_BLOCKS):
+                nc.scalar.copy(out=result[:, m, :], in_=accs[m])
+            nc.sync.dma_start(out=out_rows[:, :, WIDE], in_=result[:])
+
+        def output_middle():
+            result = sbuf([P, ROW_BLOCKS, P], F32, "result1")
+            acc = bank([P, ROW_BLOCKS, P], "o_mid", "x0")
+            passes = (with_z, with_h, with_y)
+            for m in range(ROW_BLOCKS):
+                for i, (w_q, v_q) in enumerate(passes):
+                    matmul_mx(
+                        acc[:, m, :], w_q, block(m), v_q, MIDDLE, i == 0, i == len(passes) - 1
+                    )
+            nc.scalar.copy(out=result[:], in_=acc[:])
+            nc.sync.dma_start(out=out_rows[:, :, MIDDLE], in_=result[:])
+
+        def output_last():
+            result = sbuf([P, ROW_BLOCKS, P], F32, "result2")
+            accs = products_in_four_banks(2, LAST, (with_y, with_h, with_z))
+            for m in range(ROW_BLOCKS):
+                if m % 2 == 0:
+                    nc.scalar.copy(out=result[:, m, :], in_=accs[m])
+                else:
+                    nc.vector.tensor_copy(out=result[:, m, :], in_=accs[m])
+            nc.sync.dma_start(out=out_rows[:, 0:2, LAST], in_=result[:, 0:2, :])
+            nc.scalar.dma_start(out=out_rows[:, 2:4, LAST], in_=result[:, 2:4, :])
+
+        z_wide = z_by_transposes(0, WIDE, "cd0", "h_half1")
+        quantize(z_q, WIDE, z_wide[:])
+        z_middle = z_by_transposes(1, MIDDLE, "h_half0", "z_rows1")
+        output_wide()
+        quantize(z_q, MIDDLE, z_middle[:])
+        output_middle()
+        z_last = z_on_vector(2, LAST, "z_bf0", "z_bf1")
+        quantize(z_q, LAST, z_last[:])
+        output_last()

from contextlib import ExitStack

import concourse.mybir as mybir
from concourse.masks import make_identity

K, T, S, N, H = 512, 2048, 512, 512, 512
FLOPS = 2 * K * H * S + 3 * 2 * H * N * S

F32 = mybir.dt.float32
BF16 = mybir.dt.bfloat16
I32 = mybir.dt.int32
U32 = mybir.dt.uint32
U16 = mybir.dt.uint16
U8 = mybir.dt.uint8
FP8X4 = mybir.dt.float8_e4m3fn_x4
MULT = mybir.AluOpType.mult
ADD = mybir.AluOpType.add
SUBTRACT = mybir.AluOpType.subtract
COPY = mybir.ActivationFunctionType.Copy

P = 128
PACK = 4
GROUP = 16
HALF = S // 2
ROW_BLOCKS = N // P
TURNED_PLANES = (0, 1)
WIDE, MIDDLE, LAST = slice(0, 256), slice(256, 384), slice(384, 512)


def tile_picked_cheb3_none_p_kernel(
    tc, x_words, x_scales, w1, ga, gb, w2, w3, w4, offs, p1, p2, out
):
    nc = tc.nc
    with ExitStack() as ctx:
        lists = ctx.enter_context(tc.tile_pool(name="lists", bufs=1))
        sb = ctx.enter_context(tc.tile_pool(name="sb", bufs=1))
        ps = ctx.enter_context(tc.psum_pool(name="ps", bufs=1))

        def sbuf(shape, dtype, name, tag=None):
            return sb.tile(shape, dtype, name=name, tag=tag or name, align_bytes=64)

        def bank(shape, name, tag):
            return ps.tile(shape, F32, name=name, tag=tag, bufs=1)

        def entries(list_tile, nodes):
            return list_tile[:, nodes.start // GROUP : nodes.stop // GROUP]

        def block(b, start=0):
            return slice(start + P * b, start + P * (b + 1))

        def operand(name):
            return sbuf([P, S], U32, name + "_codes"), sbuf([P, S], U8, name + "_scales")

        def quantize(packed, cols, values):
            codes, scales = packed
            nc.vector.quantize_mx(
                out=codes[:, cols].bitcast(FP8X4), scales=scales[:, cols], in_=values
            )

        def matmul_mx(acc, lhs, lhs_cols, rhs, rhs_cols, start, stop):
            nc.tensor.matmul_mx(
                out=acc,
                lhsT=lhs[0][:, lhs_cols].bitcast(FP8X4),
                lhsT_scale=lhs[1][:, lhs_cols],
                rhs=rhs[0][:, rhs_cols].bitcast(FP8X4),
                rhs_scale=rhs[1][:, rhs_cols],
                start=start,
                stop=stop,
            )

        def as_interleaved(tile):
            return tile.rearrange("p (c i t) -> p c t i", i=2, t=PACK)

        def as_planes(tile):
            return tile.rearrange("p t (c i) -> p c t i", i=2)

        def transposed_sum(acc, terms):
            for i, term in enumerate(terms):
                nc.tensor.matmul(
                    acc, lhsT=term, rhs=ident[:],
                    start=(i == 0), stop=(i == len(terms) - 1), is_transpose=True,
                )

        def gather(dst, plane, list_tile, gate, nodes):
            nc.vector.tensor_tensor(
                dst, plane[:].indirect(entries(list_tile, nodes)), gate[:, nodes], MULT
            )

        xs_win = sbuf([P, T], U8, "xs_win")
        nc.vector.memset(xs_win[:].bitcast(I32), 0)
        for q in range(4):
            nc.sync.dma_start(
                out=xs_win[32 * q : 32 * q + 4, :].bitcast(I32),
                in_=x_scales[0, 4 * q : 4 * q + 4, :].bitcast(I32),
            )
        offs_t = lists.tile([P, S // GROUP], U16, name="offs_t")
        nc.sync.dma_start(offs_t[:], offs)
        w1_raw = sbuf([P, PACK, H], F32, "w1_raw")
        nc.sync.dma_start(out=w1_raw[:], in_=w1.rearrange("(p j) c -> p j c", j=PACK))
        p1_t = lists.tile([P, S // GROUP], U16, name="p1_t")
        nc.sync.dma_start(p1_t[:], p1)
        p2_t = lists.tile([P, S // GROUP], U16, name="p2_t")
        nc.sync.dma_start(p2_t[:], p2)
        xw_win = sbuf([P, T], U32, "xw_win")
        nc.sync.dma_start(
            out=xw_win[:].bitcast(I32),
            in_=x_words[0].rearrange("p n t -> p (n t)").bitcast(I32),
        )
        ga_t = sbuf([P, S], F32, "ga_t")
        nc.sync.dma_start(out=ga_t[:], in_=ga)
        gb_t = sbuf([P, S], F32, "gb_t")
        nc.sync.dma_start(out=gb_t[:], in_=gb)
        w_raw = {}
        for name, w in (("w2", w2), ("w3", w3), ("w4", w4)):
            raw = sbuf([P, PACK, N], F32, name + "_raw")
            nc.sync.dma_start(out=raw[:], in_=w.rearrange("(p j) c -> p j c", j=PACK))
            w_raw.setdefault(name, raw)

        ident = sbuf([P, P], F32, "ident")
        make_identity(nc, ident[:])

        all_nodes = slice(0, S)
        halves = (slice(0, HALF), slice(HALF, S))
        x_q = operand("x")
        nc.vector.tensor_copy(x_q[1][:], xs_win[:].indirect(offs_t[:]))

        w1_q = operand("w1")
        w1_view = w1_raw[:].rearrange("p j (m t) -> p m t j", t=PACK)
        w1_bf = [sbuf([P, 2 * P * PACK], BF16, "w1_bf%d" % u) for u in range(2)]
        w1_bf_view = [b[:].rearrange("p (t m j) -> p m t j", t=2, j=PACK) for b in w1_bf]
        nc.vector.tensor_copy(out=w1_bf_view[0], in_=w1_view[:, :, 0:2, :])
        nc.scalar.activation(out=w1_bf_view[1], in_=w1_view[:, :, 2:4, :], func=COPY)
        for u in range(2):
            quantize(w1_q, slice(2 * P * u, 2 * P * (u + 1)), w1_bf[u][:])

        for nodes in halves:
            nc.vector.tensor_copy(x_q[0][:, nodes], xw_win[:].indirect(entries(offs_t, nodes)))

        y_win = [sbuf([P, 2 * S], F32, "y_win%d" % t) for t in range(PACK)]
        for t in range(PACK):
            nc.vector.memset(y_win[t][:, S:], 0.0)
        y_all = sbuf([P, PACK, S], F32, "y_all")
        for t in range(PACK):
            acc = bank([P, S], "y_acc%d" % t, "o%d" % t)
            if t == 0:
                early = bank([P, S], "y_early", "x0")
                pieces = ((halves[0], early), (halves[1], acc))
            else:
                pieces = ((all_nodes, acc),)
            for nodes, piece in pieces:
                matmul_mx(piece[:, nodes], w1_q, block(t), x_q, nodes, True, True)
                nc.scalar.copy(out=y_win[t][:, nodes], in_=piece[:, nodes])
            nc.sync.dma_start(out=y_all[:, t, :], in_=y_win[t][:, all_nodes])

        gb_scaled = sbuf([P, S], F32, "gb_z")
        nc.vector.tensor_scalar(gb_scaled[:], gb_t[:], -2.0, None, MULT)

        h_win = [sbuf([P, S], F32, "h_win%d" % t) for t in range(PACK)]
        h_half = [sbuf([P, PACK, HALF], F32, "h_half%d" % i) for i in range(2)]
        first = []
        second = [sbuf([P, S], F32, "second%d" % t) for t in range(PACK)]

        def weight(name, number):
            values = sbuf([P, N * PACK], BF16, "w_bf%d" % number, tag=name + "_bf")
            nc.scalar.copy(out=as_interleaved(values[:]), in_=as_planes(w_raw[name][:]))
            packed = operand(name)
            quantize(packed, slice(0, N), values[:])
            return packed

        def add_h(t):
            if t in TURNED_PLANES:
                turned = bank([P, S], "h_turned%d" % t, "x%d" % (2 * t))
                for b in range(S // P):
                    cols = block(b)
                    transposed_sum(turned[:, cols], (first[t][:, cols], second[t][:, cols]))
                rows = sbuf([P, S], F32, "h_rows%d" % t, tag=("rows0", "w2_raw")[t])
                nc.scalar.activation(out=rows[:], in_=turned[:], func=COPY, scale=-2.0)
                back = bank([P, S], "h_back%d" % t, "x%d" % (2 * t + 1))
                for b in range(S // P):
                    nc.tensor.transpose(back[:, block(b)], rows[:, block(b)], ident[:])
                nc.scalar.copy(out=h_win[t][:], in_=back[:])
            else:
                nc.vector.scalar_tensor_tensor(
                    h_win[t][:], first[t][:], -2.0, second[t][:], MULT, ADD
                )
            queue = nc.scalar if t == 0 else nc.sync
            for i in range(2):
                queue.dma_start(out=h_half[i][:, t, :], in_=h_win[t][:, halves[i]])

        def gather_y(t):
            first.append(sbuf([P, S], F32, "first%d" % t))
            gather(first[t][:], y_win[t], p1_t, ga_t, all_nodes)
            if t > 0:
                add_h(t - 1)
            gate = gb_t if t in TURNED_PLANES else gb_scaled
            gather(second[t][:], y_win[t], p2_t, gate, all_nodes)

        gather_y(0)
        w2_q = weight("w2", 0)
        gather_y(1)
        w3_q = weight("w3", 1)
        gather_y(2)
        gather_y(3)
        add_h(3)
        w4_q = weight("w4", 2)

        y_bf = sbuf([P, S * PACK], BF16, "y_bf", tag="w2_raw")
        nc.scalar.copy(out=as_interleaved(y_bf[:]), in_=as_planes(y_all[:]))
        y_q = operand("y")
        quantize(y_q, all_nodes, y_bf[:])

        h_q = operand("h")
        z_q = operand("z")
        for i in range(2):
            h_bf = sbuf([P, HALF * PACK], BF16, "h_bf%d" % i)
            nc.scalar.activation(
                out=as_interleaved(h_bf[:]), in_=as_planes(h_half[i][:]), func=COPY, scale=-0.5
            )
            quantize(h_q, halves[i], h_bf[:])

        def terms_of_z(number, nodes, tag):
            both = sbuf([P, 2, PACK, nodes.stop - nodes.start], F32, "cd%d" % number, tag=tag)
            return both[:, 0], both[:, 1]

        def z_by_transposes(number, nodes, terms_tag, rows_tag):
            blocks = (nodes.stop - nodes.start) // P
            by_p1, by_p2 = terms_of_z(number, nodes, terms_tag)
            z_rows = sbuf([P, blocks, 2, 2 * P], BF16, "z_rows%d" % number, tag=rows_tag)
            words = bank([P, blocks, 2, P], "words%d" % number, "x1")
            for u in (1, 0):
                minus_z = bank([P, blocks, 2, P], "zt%d_%d" % (number, u), "x%d" % (3 - u))
                for e in range(2):
                    t = 2 * u + e
                    gather(by_p2[:, t, :], h_win[t], p2_t, gb_t, nodes)
                    gather(by_p1[:, t, :], h_win[t], p1_t, ga_t, nodes)
                    for b in range(blocks):
                        transposed_sum(
                            minus_z[:, b, e, :],
                            (
                                y_win[t][:, block(b, nodes.start)],
                                by_p2[:, t, block(b)],
                                by_p1[:, t, block(b)],
                            ),
                        )
                nc.scalar.activation(
                    out=z_rows[:, :, u, :].rearrange("j b (p e) -> j b p e", e=2),
                    in_=minus_z[:].rearrange("j b e p -> j b p e"),
                    func=COPY,
                    scale=-1.0,
                )
                for b in range(blocks):
                    nc.tensor.transpose(
                        words[:, b, u, :], z_rows[:, b, u, :].bitcast(F32), ident[:]
                    )
            z_bf = sbuf([P, blocks * P * PACK], BF16, "z_bf%d" % number)
            nc.scalar.copy(
                out=z_bf[:].bitcast(F32).rearrange("p (b j u) -> p b j u", b=blocks, u=2),
                in_=words[:].rearrange("p b u j -> p b j u"),
            )
            return z_bf

        def z_on_vector(number, nodes, terms_tag, z_tag):
            width = nodes.stop - nodes.start
            by_p1, by_p2 = terms_of_z(number, nodes, terms_tag)
            for t in range(PACK):
                gather(by_p2[:, t, :], h_win[t], p2_t, gb_t, nodes)
            gather(by_p1[:, 0, :], h_win[0], p1_t, ga_t, nodes)
            partial = sbuf([P, PACK, width], F32, "partial")
            nc.vector.scalar_tensor_tensor(
                partial[:], by_p2, -1.0, y_all[:, :, nodes], MULT, SUBTRACT
            )
            for t in range(1, PACK):
                gather(by_p1[:, t, :], h_win[t], p1_t, ga_t, nodes)
            z_bf = sbuf([P, width * PACK], BF16, "z_bf%d" % number, tag=z_tag)
            nc.vector.tensor_tensor(
                as_interleaved(z_bf[:]), as_planes(partial[:]), as_planes(by_p1), SUBTRACT
            )
            return z_bf

        with_y, with_h, with_z = (w2_q, y_q), (w3_q, h_q), (w4_q, z_q)
        out_rows = out.rearrange("(m p) j -> p m j", p=P)

        def products_in_four_banks(number, nodes, passes):
            width = nodes.stop - nodes.start
            accs = [
                bank([P, S], "o_acc%d_%d" % (number, m), "o%d" % m)[:, :width]
                for m in range(ROW_BLOCKS)
            ]
            for i, (w_q, v_q) in enumerate(passes):
                for m in range(ROW_BLOCKS):
                    matmul_mx(accs[m], w_q, block(m), v_q, nodes, i == 0, i == len(passes) - 1)
            return accs

        def output_wide():
            result = sbuf([P, ROW_BLOCKS, WIDE.stop - WIDE.start], F32, "result0")
            accs = products_in_four_banks(0, WIDE, (with_y, with_z, with_h))
            for m in range(ROW_BLOCKS):
                nc.scalar.copy(out=result[:, m, :], in_=accs[m])
            nc.sync.dma_start(out=out_rows[:, :, WIDE], in_=result[:])

        def output_middle():
            result = sbuf([P, ROW_BLOCKS, P], F32, "result1")
            acc = bank([P, ROW_BLOCKS, P], "o_mid", "x0")
            passes = (with_z, with_h, with_y)
            for m in range(ROW_BLOCKS):
                for i, (w_q, v_q) in enumerate(passes):
                    matmul_mx(
                        acc[:, m, :], w_q, block(m), v_q, MIDDLE, i == 0, i == len(passes) - 1
                    )
            nc.scalar.copy(out=result[:], in_=acc[:])
            nc.sync.dma_start(out=out_rows[:, :, MIDDLE], in_=result[:])

        def output_last():
            result = sbuf([P, ROW_BLOCKS, P], F32, "result2")
            accs = products_in_four_banks(2, LAST, (with_y, with_h, with_z))
            for m in range(ROW_BLOCKS):
                if m % 2 == 0:
                    nc.scalar.copy(out=result[:, m, :], in_=accs[m])
                else:
                    nc.vector.tensor_copy(out=result[:, m, :], in_=accs[m])
            nc.sync.dma_start(out=out_rows[:, 0:2, LAST], in_=result[:, 0:2, :])
            nc.scalar.dma_start(out=out_rows[:, 2:4, LAST], in_=result[:, 2:4, :])

        z_wide = z_by_transposes(0, WIDE, "cd0", "h_half1")
        quantize(z_q, WIDE, z_wide[:])
        z_middle = z_by_transposes(1, MIDDLE, "h_half0", "z_rows1")
        output_wide()
        quantize(z_q, MIDDLE, z_middle[:])
        output_middle()
        z_last = z_on_vector(2, LAST, "z_bf0", "z_bf1")
        quantize(z_q, LAST, z_last[:])
        output_last()
